import numpy as np
import ml_dtypes


def mxq(x, axis, fmt="e4m3"):
    dtype, down = {"e4m3": (ml_dtypes.float8_e4m3fn, 7), "e5m2": (ml_dtypes.float8_e5m2, 14)}[fmt]
    v = np.moveaxis(np.asarray(x, np.float32).astype(ml_dtypes.bfloat16).astype(np.float64), axis, -1)
    blocks = v.reshape(v.shape[:-1] + (-1, 32))
    amax = np.abs(blocks).max(-1, keepdims=True)
    byte = np.maximum(np.where(amax > 0, np.frexp(amax)[1] - 1 + 127, 0) - down, 1)
    scale = np.exp2(byte - 127.0)
    codes = (blocks / scale).astype(np.float32).astype(dtype).astype(np.float64)
    return np.moveaxis((codes * scale).reshape(v.shape), -1, axis)


WIDE = False


def mx_kscale(k):
    if not WIDE:
        return np.ones(k)
    levels = np.array([10, -10, 5, -5, 0])
    if k % 512:
        return np.exp2(np.random.permutation(np.resize(levels, k // 32))).repeat(32)
    a = np.empty((k // 512, 16))
    for p in range(k // 512):
        a[p, :8] = np.random.permutation(np.resize(levels, 8))
        for g in range(8):
            far = levels[np.abs(levels - a[p, g]) >= 10]
            a[p, g + 8] = far[np.random.randint(len(far))]
    return np.exp2(a.ravel()).repeat(32)


def f64(x):
    return np.asarray(x).astype(np.float64)


def striped(idx):
    return np.tile(np.asarray(idx).reshape(-1, 16).T, (8, 1)).astype(np.uint16)


def unstriped(offs):
    return offs[:16].T.reshape(-1).astype(np.int64)


E2M1 = np.array([0.0, 0.5, 1.0, 1.5, 2.0, 3.0, 4.0, 6.0, -0.0, -0.5, -1.0, -1.5, -2.0, -3.0, -4.0, -6.0])


def pack_weight(w, fmt):
    k, n = w.shape
    w = f64(np.asarray(w, np.float32).astype(ml_dtypes.bfloat16)).reshape(k // 32, 32, n)
    amax = np.abs(w).max(1)
    if fmt == "e4m3":
        byte = np.frexp(amax)[1] - 1 + 127 - 7
    else:
        mant, ex = np.frexp(amax / 6.0)
        byte = np.where(mant > 0.5, ex, ex - 1) + 127
    byte = np.clip(np.where(amax > 0, byte, 1), 1, 254)
    scaled = (w * np.exp2(127.0 - byte)[:, None, :]).reshape(k, n).astype(np.float32)
    by_word = np.ascontiguousarray(scaled.reshape(k // 512, 128, 4, n).transpose(0, 1, 3, 2))
    if fmt == "e4m3":
        words = by_word.astype(ml_dtypes.float8_e4m3fn).view(np.uint8)
    else:
        c = by_word.astype(ml_dtypes.float4_e2m1fn).view(np.uint8) & 0xF
        words = (c[..., 0::2] | (c[..., 1::2] << 4)).reshape(k // 512, 128, 2 * n)
    return np.ascontiguousarray(words), np.ascontiguousarray(byte.astype(np.uint8).reshape(k // 512, 16, n))


def unpack_weight(words, scales, fmt):
    g, _, n = scales.shape
    words = np.ascontiguousarray(words).reshape(g, 128, n, -1)
    if fmt == "e4m3":
        vals = words.view(ml_dtypes.float8_e4m3fn).astype(np.float64)
    else:
        nib = np.empty((g, 128, n, 4), np.uint8)
        nib[..., 0::2] = words & 0xF
        nib[..., 1::2] = words >> 4
        vals = E2M1[nib]
    vals = vals * np.repeat(np.exp2(scales.astype(np.float64) - 127.0), 8, axis=1)[..., None]
    return vals.transpose(0, 1, 3, 2).reshape(g * 512, n)


def bf(x):
    return np.asarray(x, np.float32).astype(ml_dtypes.bfloat16)


def planes(Y):
    r, m = Y.shape
    b = f64(bf(Y)).reshape(r // 32, 32, m)
    amax = np.abs(b).max(1)
    byte = np.clip(np.where(amax > 0, np.frexp(amax)[1] - 1 + 127 - 7, 1), 1, 254)
    codes = (b * np.exp2(127.0 - byte)[:, None, :]).reshape(r, m).astype(np.float32).astype(ml_dtypes.float8_e4m3fn).view(np.uint8)
    words = codes.reshape(r // 512, 128, 4, m).transpose(0, 1, 3, 2)
    return np.ascontiguousarray(words), np.ascontiguousarray(byte.astype(np.uint8).reshape(r // 512, 16, m))


B, N, T, D, NQ = 1, 512, 2048, 512, 512


def setup_inputs():
    n = np.random.standard_normal
    idx = np.random.permutation(T)[:B * N]
    s = mx_kscale(D)[:, None]
    kp = pack_weight(n((D, T)) / s, "e4m3")
    return {
        "qT": (n((B, D, NQ)) * s * (1.00 / np.sqrt(D))).astype(np.float32),
        "k_words": kp[0],
        "k_scales": kp[1],
        "ps": np.tile(np.random.randint(0, 64, 2048), (128, 1)).astype(np.float32),
        "sl": (np.random.uniform(0.01, 0.05, (B, 1, NQ))).astype(np.float32),
        "pq": (np.random.randint(0, 64, (B, 1, NQ))).astype(np.float32),
        "ls": (np.random.uniform(7.8, 8.4, (B, 1, NQ))).astype(np.float32),
        "offs": striped(idx),
    }


def reference(qT, k_words, k_scales, ps, sl, pq, ls, offs):
    idx = unstriped(offs)
    pick = lambda x, which: x[:, which].reshape(x.shape[0], B, -1).transpose(1, 0, 2)
    k = unpack_weight(k_words, k_scales, "e4m3")
    kg = pick(k, idx)
    qq = mxq(f64(qT), 1, "e4m3")
    a = kg.transpose(0, 2, 1) @ qq
    y = np.exp(a - f64(sl) * np.abs(pick(f64(ps), idx)[:, :1, :].transpose(0, 2, 1) - f64(pq)) - f64(ls))
    Y = y[0]
    words, scales = planes(Y)
    return Y, words, scales

@@ -1,0 +1,143 @@
+from contextlib import ExitStack
+
+import concourse.mybir as mybir
+
+F32 = mybir.dt.float32
+BF16 = mybir.dt.bfloat16
+I32 = mybir.dt.int32
+U32 = mybir.dt.uint32
+U16 = mybir.dt.uint16
+U8 = mybir.dt.uint8
+FP8X4 = mybir.dt.float8_e4m3fn_x4
+ACT = mybir.ActivationFunctionType
+ALU = mybir.AluOpType
+
+P = 128
+PACK = 4
+N, T, D, NQ = 512, 2048, 512, 512
+QB = 128
+NB = NQ // QB
+FLOPS = 2 * N * D * NQ
+
+
+def tile_attend_plw_alibi_topk_kernel(tc, qT, k_words, k_scales, ps, sl, pq, ls, offs, out_0, out_1, out_2):
+    nc = tc.nc
+    with ExitStack() as ctx:
+        sb = ctx.enter_context(tc.tile_pool(name="sb", bufs=1))
+        late = ctx.enter_context(tc.tile_pool(name="late", bufs=1))
+        psum = ctx.enter_context(tc.psum_pool(name="psum", bufs=1))
+
+        offsets = sb.tile([P, N // 16], U16, name="offsets")
+        ks_win = sb.tile([P, T], U8, name="ks_win", align_bytes=64)
+        ps_win = sb.tile([P, T], F32, name="ps_win", align_bytes=64)
+        rows = sb.tile([P, P], F32, name="rows")
+        ident = sb.tile([P, P], F32, name="ident")
+        warm = sb.tile([P, 8], F32, name="warm")
+        zeros = late.tile([P, P], F32, name="zeros", offset=4 * T - 2 * P)
+
+        nc.vector.memset(ks_win[:].bitcast(I32), 0)
+        nc.vector.memset(ps_win[:].bitcast(I32), 0)
+        nc.gpsimd.memset(rows[:], 0.0)
+        nc.vector.memset(zeros[:], 0.0)
+        nc.gpsimd.affine_select(out=ident[:], in_=zeros[:], compare_op=ALU.not_equal, fill=1.0, base=0,
+                                pattern=[[-1, P]], channel_multiplier=1)
+        nc.scalar.activation(warm[64:128, :], rows[64:128, 0:8], ACT.Exp)
+        kw_win = late.tile([P, T], I32, name="kw_win", offset=0)
+
+        q_src = qT[0].rearrange("(p j) w -> p j w", j=PACK)
+        HALF = NQ // 2
+        q_raw = [sb.tile([P, PACK, HALF], F32, name="q_raw0"),
+                 late.tile([P, PACK, HALF], F32, name="q_raw1", offset=4 * T)]
+
+        nc.sync.dma_start(offsets[:], offs)
+        nc.sync.dma_start(q_raw[0][:], q_src[:, :, 0:HALF])
+        nc.sync.dma_start(ks_win[:].bitcast(I32)[0:16, :], k_scales[0].bitcast(I32))
+        for i, vec in enumerate((pq, sl, ls)):
+            nc.sync.dma_start(rows[NB * i : NB * (i + 1), :], vec[0].rearrange("o (c m) -> (o c) m", m=QB))
+        nc.sync.dma_start(ps_win[0:1, :], ps[0:1, :])
+        nc.sync.dma_start(kw_win[:], k_words[0].rearrange("p t r -> p (t r)").bitcast(I32))
+        nc.sync.dma_start(q_raw[1][:], q_src[:, :, HALF:NQ])
+
+        rows_t = psum.tile([P, N], F32, name="rows_t", tag="f0")
+        nc.tensor.transpose(rows_t[:, 0:P], rows[:], ident[:])
+        cols = sb.tile([P, 3 * NB], F32, name="cols")
+        nc.scalar.copy(cols[:], rows_t[:, 0 : 3 * NB])
+
+        ks_g = sb.tile([P, N], U8, name="ks_g", align_bytes=64)
+        nc.vector.tensor_copy(ks_g[:], ks_win[:].indirect(offsets[:]))
+        ks_plane = sb.tile([P, N], U8, name="ks_plane", align_bytes=64)
+        nc.vector.tensor_copy(ks_plane[:].bitcast(I32), ks_g[:].bitcast(I32))
+        for quad in range(1, 4):
+            nc.scalar.dma_start(ks_plane[:].bitcast(I32)[32 * quad : 32 * quad + 4, :],
+                                ks_g[:].bitcast(I32)[4 * quad : 4 * quad + 4, :])
+        ps_g = sb.tile([P, N], F32, name="ps_g")
+        nc.vector.tensor_copy(ps_g[:], ps_win[:].indirect(offsets[:]))
+        q_mx = []
+        for j in range(NB):
+            h, c0 = divmod(j * QB, HALF)
+            qb = sb.tile([P, QB, PACK], BF16, name=f"qb{j}", align_bytes=64)
+            nc.scalar.copy(qb[:].rearrange("p (c i) t -> p c t i", i=4),
+                           q_raw[h][:, :, c0 : c0 + QB].rearrange("p t (c i) -> p c t i", i=4))
+            qw = sb.tile([P, QB], U32, name=f"qw{j}", align_bytes=64)
+            qs = sb.tile([P, QB], U8, name=f"qs{j}", align_bytes=64)
+            nc.vector.quantize_mx(out=qw[:].bitcast(FP8X4), scales=qs[:], in_=qb[:].rearrange("p c t -> p (c t)"))
+            q_mx.append((qw, qs))
+
+        kw_g = sb.tile([P, N], U32, name="kw_g", align_bytes=64)
+        nc.vector.tensor_copy(kw_g[:], kw_win[:].bitcast(U32).indirect(offsets[:]))
+
+        ps_t = psum.tile([P, N // P, P], F32, name="ps_t", tag="f1")
+        for c in range(N // P):
+            nc.tensor.transpose(ps_t[:, c, :], ps_g[:, c * P : (c + 1) * P], ident[:])
+        ps_col = sb.tile([P, N // P], F32, name="ps_col")
+        nc.scalar.copy(ps_col[:], ps_t[:, :, 0])
+        ps_bc = psum.tile([P, N], F32, name="ps_bc", tag="f2")
+        for c in range(N // P):
+            nc.tensor.transpose(ps_bc[:, c * P : (c + 1) * P], ps_col[:, c : c + 1].to_broadcast([P, P]), ident[:])
+
+        dist = []
+        for j in range(NB):
+            d = sb.tile([P, PACK, P], F32, name=f"dist{j}")
+            nc.scalar.activation(d[:], ps_bc[:].rearrange("q (s r) -> q r s", r=PACK), ACT.Abs,
+                                 bias=cols[:, j : j + 1], scale=-1.0)
+            dist.append(d)
+
+        acc = []
+        for j in range(NB):
+            o = psum.tile([P, PACK, QB], F32, name=f"acc{j}", tag=f"o{j}")
+            ls_col = cols[:, 2 * NB + j : 2 * NB + j + 1].to_broadcast([P, P])
+            for r in range(PACK):
+                nc.tensor.matmul(o[:, r, :], ls_col, ident[:], is_transpose=True, start=(r == 0), stop=False)
+            acc.append(o)
+
+        y_words = sb.tile([P, NQ], U32, name="y_words", align_bytes=64)
+        y_scales = sb.tile([P, NQ], U8, name="y_scales", align_bytes=64)
+        out_rows = out_0.rearrange("(s r) q -> s r q", r=PACK)
+        out_words = out_1[0].rearrange("p q u -> p (q u)").bitcast(I32)
+        score_tags = ("f0", "f3", "f1", "f2")
+
+        for j in range(NB):
+            cs = slice(j * QB, (j + 1) * QB)
+            qw, qs = q_mx[j]
+            a = psum.tile([P, N], F32, name=f"a{j}", tag=score_tags[j])
+            nc.tensor.matmul_mx(out=a[:], lhsT=qw[:].bitcast(FP8X4), lhsT_scale=qs[:],
+                                rhs=kw_g[:].bitcast(FP8X4), rhs_scale=ks_plane[:], start=True, stop=True)
+            z = sb.tile([P, PACK, P], F32, name=f"z{j}")
+            nc.vector.scalar_tensor_tensor(z[:], dist[j][:], cols[:, NB + j : NB + j + 1],
+                                           a[:].rearrange("q (s r) -> q r s", r=PACK), ALU.mult, ALU.subtract)
+            for r in range(PACK):
+                nc.tensor.matmul(acc[j][:, r, :], z[:, r, :], ident[:], is_transpose=True, start=False,
+                                 stop=(r == PACK - 1))
+            y = sb.tile([P, PACK, QB], F32, name=f"y{j}")
+            nc.scalar.activation(y[:], acc[j][:], ACT.Exp, scale=-1.0)
+            nc.sync.dma_start(out_rows[:, :, cs], y[:])
+            yb = sb.tile([P, QB, PACK], BF16, name=f"yb{j}", align_bytes=64)
+            nc.vector.tensor_copy(yb[:].rearrange("p (c i) t -> p c t i", i=4),
+                                  y[:].rearrange("p t (c i) -> p c t i", i=4))
+            nc.vector.quantize_mx(out=y_words[:, cs].bitcast(FP8X4), scales=y_scales[:, cs],
+                                  in_=yb[:].rearrange("p c t -> p (c t)"))
+            nc.sync.dma_start(out_words[:, cs], y_words[:, cs].bitcast(I32))
+        for quad in range(4):
+            eng = nc.scalar if quad % 2 else nc.sync
+            eng.dma_start(out_2[0, 4 * quad : 4 * quad + 4, :].bitcast(I32),
+                          y_scales[:].bitcast(I32)[32 * quad : 32 * quad + 4, :])

@@ -17,6 +17,7 @@ PACK = 4
 N, T, D, NQ = 512, 2048, 512, 512
 QB = 128
 NB = NQ // QB
+HALF = NQ // 2
 FLOPS = 2 * N * D * NQ
 
 
@@ -27,85 +28,102 @@ def tile_attend_plw_alibi_topk_kernel(tc, qT, k_words, k_scales, ps, sl, pq, ls,
         late = ctx.enter_context(tc.tile_pool(name="late", bufs=1))
         psum = ctx.enter_context(tc.psum_pool(name="psum", bufs=1))
 
+        AT_KS, AT_PS, AT_KW, AT_DIST = 0, 2 * T, 6 * T, 10 * T
         offsets = sb.tile([P, N // 16], U16, name="offsets")
-        ks_win = sb.tile([P, T], U8, name="ks_win", align_bytes=64)
-        ps_win = sb.tile([P, T], F32, name="ps_win", align_bytes=64)
+        ks_win = late.tile([P, T], U8, name="ks_win", offset=AT_KS, align_bytes=64)
+        ps_win = late.tile([P, T], F32, name="ps_win", offset=AT_PS)
+        kw_win = late.tile([P, T], I32, name="kw_win", offset=AT_KW)
         rows = sb.tile([P, P], F32, name="rows")
         ident = sb.tile([P, P], F32, name="ident")
         warm = sb.tile([P, 8], F32, name="warm")
-        zeros = late.tile([P, P], F32, name="zeros", offset=4 * T - 2 * P)
-
-        nc.vector.memset(ks_win[:].bitcast(I32), 0)
-        nc.vector.memset(ps_win[:].bitcast(I32), 0)
-        nc.gpsimd.memset(rows[:], 0.0)
-        nc.vector.memset(zeros[:], 0.0)
-        nc.gpsimd.affine_select(out=ident[:], in_=zeros[:], compare_op=ALU.not_equal, fill=1.0, base=0,
-                                pattern=[[-1, P]], channel_multiplier=1)
-        nc.scalar.activation(warm[64:128, :], rows[64:128, 0:8], ACT.Exp)
-        kw_win = late.tile([P, T], I32, name="kw_win", offset=0)
-
+        ks_plane = sb.tile([P, N], U8, name="ks_plane", align_bytes=64)
         q_src = qT[0].rearrange("(p j) w -> p j w", j=PACK)
-        HALF = NQ // 2
-        q_raw = [sb.tile([P, PACK, HALF], F32, name="q_raw0"),
-                 late.tile([P, PACK, HALF], F32, name="q_raw1", offset=4 * T)]
+        q_raw = [sb.tile([P, PACK, HALF], F32, name="q_raw0")]
+        KS0 = 48
+        ROW0 = P - 3 * NB
+        CUT = 3 * T // 4
 
         nc.sync.dma_start(offsets[:], offs)
-        nc.sync.dma_start(q_raw[0][:], q_src[:, :, 0:HALF])
-        nc.sync.dma_start(ks_win[:].bitcast(I32)[0:16, :], k_scales[0].bitcast(I32))
-        for i, vec in enumerate((pq, sl, ls)):
-            nc.sync.dma_start(rows[NB * i : NB * (i + 1), :], vec[0].rearrange("o (c m) -> (o c) m", m=QB))
-        nc.sync.dma_start(ps_win[0:1, :], ps[0:1, :])
+        nc.sync.dma_start(ks_win[:].bitcast(I32)[KS0 : KS0 + 16, :], k_scales[0].bitcast(I32))
+        nc.sync.dma_start(ps_win[P - 1 : P, :], ps[0:1, :])
+        for i, vec in enumerate((ls, pq, sl)):
+            nc.scalar.dma_start(rows[ROW0 + NB * i : ROW0 + NB * (i + 1), :],
+                                vec[0].rearrange("o (c m) -> (o c) m", m=QB))
         nc.sync.dma_start(kw_win[:], k_words[0].rearrange("p t r -> p (t r)").bitcast(I32))
-        nc.sync.dma_start(q_raw[1][:], q_src[:, :, HALF:NQ])
+        nc.sync.dma_start(q_raw[0][:], q_src[:, :, 0:HALF])
 
-        rows_t = psum.tile([P, N], F32, name="rows_t", tag="f0")
+        nc.vector.memset(ks_win[:].bitcast(I32)[0:KS0, :], 0)
+        nc.vector.memset(ps_win[0 : P - 1, 0:CUT], 0.0)
+        nc.gpsimd.memset(rows[0:ROW0, :], 0.0)
+        nc.gpsimd.memset(ident[:], 0.0)
+        nc.gpsimd.affine_select(out=ident[:], in_=ident[:], compare_op=ALU.not_equal, fill=1.0, base=0,
+                                pattern=[[-1, P]], channel_multiplier=1)
+        nc.gpsimd.memset(ks_win[:].bitcast(I32)[64:P, :], 0)
+        nc.gpsimd.memset(ps_win[0 : P - 1, CUT:T], 0.0)
+        nc.gpsimd.memset(ks_plane[:].bitcast(I32), 0)
+        nc.scalar.activation(warm[0:64, :], rows[0:64, 0:8], ACT.Exp)
+
+        rows_t = psum.tile([P, N], F32, name="rows_t", tag="b0")
         nc.tensor.transpose(rows_t[:, 0:P], rows[:], ident[:])
         cols = sb.tile([P, 3 * NB], F32, name="cols")
-        nc.scalar.copy(cols[:], rows_t[:, 0 : 3 * NB])
+        nc.vector.tensor_copy(cols[:], rows_t[:, ROW0:P])
 
+        ps_g = sb.tile([P, N], F32, name="ps_g")
+        nc.scalar.activation(ps_g[:], ps_win[:].indirect(offsets[:]), ACT.Copy)
         ks_g = sb.tile([P, N], U8, name="ks_g", align_bytes=64)
         nc.vector.tensor_copy(ks_g[:], ks_win[:].indirect(offsets[:]))
-        ks_plane = sb.tile([P, N], U8, name="ks_plane", align_bytes=64)
-        nc.vector.tensor_copy(ks_plane[:].bitcast(I32), ks_g[:].bitcast(I32))
-        for quad in range(1, 4):
-            nc.scalar.dma_start(ks_plane[:].bitcast(I32)[32 * quad : 32 * quad + 4, :],
-                                ks_g[:].bitcast(I32)[4 * quad : 4 * quad + 4, :])
-        ps_g = sb.tile([P, N], F32, name="ps_g")
-        nc.vector.tensor_copy(ps_g[:], ps_win[:].indirect(offsets[:]))
+        for quad in range(4):
+            nc.sync.dma_start(ks_plane[:].bitcast(I32)[32 * quad : 32 * quad + 4, :],
+                              ks_g[:].bitcast(I32)[KS0 + 4 * quad : KS0 + 4 * quad + 4, :])
+        q_raw.append(late.tile([P, PACK, HALF], F32, name="q_raw1", offset=AT_KS))
+        nc.sync.dma_start(q_raw[1][:], q_src[:, :, HALF:NQ])
+        kw_g = late.tile([P, N], U32, name="kw_g", offset=AT_PS, align_bytes=64)
+        nc.vector.tensor_copy(kw_g[:], kw_win[:].bitcast(U32).indirect(offsets[:]))
+
+        ps_col = []
+        for h in range(2):
+            ps_t = psum.tile([P, 2, P], F32, name=f"ps_t{h}", tag=f"o{2 + h}")
+            for c in range(2):
+                nc.tensor.transpose(ps_t[:, c, :], ps_g[:, (2 * h + c) * P : (2 * h + c + 1) * P], ident[:])
+            col = sb.tile([P, 2], F32, name=f"ps_col{h}")
+            nc.scalar.copy(col[:], ps_t[:, :, P - 1])
+            ps_col.append(col)
+        ps_bc = psum.tile([P, N], F32, name="ps_bc", tag="b2")
+        for c in range(N // P):
+            nc.tensor.transpose(ps_bc[:, c * P : (c + 1) * P],
+                                ps_col[c // 2][:, c % 2 : c % 2 + 1].to_broadcast([P, P]), ident[:])
+
+        dist = []
+        for j in range(NB):
+            d = late.tile([P, PACK, P], F32, name=f"dist{j}", offset=AT_DIST + 4 * N * j, align_bytes=64)
+            nc.scalar.activation(d[:], ps_bc[:].rearrange("q (s r) -> q r s", r=PACK), ACT.Abs,
+                                 bias=cols[:, NB + j : NB + j + 1], scale=-1.0)
+            dist.append(d)
+
         q_mx = []
         for j in range(NB):
             h, c0 = divmod(j * QB, HALF)
-            qb = sb.tile([P, QB, PACK], BF16, name=f"qb{j}", align_bytes=64)
-            nc.scalar.copy(qb[:].rearrange("p (c i) t -> p c t i", i=4),
-                           q_raw[h][:, :, c0 : c0 + QB].rearrange("p t (c i) -> p c t i", i=4))
+            qb = late.tile([P, QB, PACK], BF16, name=f"qb{j}", offset=AT_KW + 2 * N * j, align_bytes=64)
+            nc.vector.tensor_copy(qb[:].rearrange("p (c i) t -> p c t i", i=4),
+                                  q_raw[h][:, :, c0 : c0 + QB].rearrange("p t (c i) -> p c t i", i=4))
             qw = sb.tile([P, QB], U32, name=f"qw{j}", align_bytes=64)
             qs = sb.tile([P, QB], U8, name=f"qs{j}", align_bytes=64)
             nc.vector.quantize_mx(out=qw[:].bitcast(FP8X4), scales=qs[:], in_=qb[:].rearrange("p c t -> p (c t)"))
             q_mx.append((qw, qs))
 
-        kw_g = sb.tile([P, N], U32, name="kw_g", align_bytes=64)
-        nc.vector.tensor_copy(kw_g[:], kw_win[:].bitcast(U32).indirect(offsets[:]))
-
-        ps_t = psum.tile([P, N // P, P], F32, name="ps_t", tag="f1")
-        for c in range(N // P):
-            nc.tensor.transpose(ps_t[:, c, :], ps_g[:, c * P : (c + 1) * P], ident[:])
-        ps_col = sb.tile([P, N // P], F32, name="ps_col")
-        nc.scalar.copy(ps_col[:], ps_t[:, :, 0])
-        ps_bc = psum.tile([P, N], F32, name="ps_bc", tag="f2")
-        for c in range(N // P):
-            nc.tensor.transpose(ps_bc[:, c * P : (c + 1) * P], ps_col[:, c : c + 1].to_broadcast([P, P]), ident[:])
-
-        dist = []
+        score_tags = ("b3", "b1", "b0", "b2")
+        scores = []
         for j in range(NB):
-            d = sb.tile([P, PACK, P], F32, name=f"dist{j}")
-            nc.scalar.activation(d[:], ps_bc[:].rearrange("q (s r) -> q r s", r=PACK), ACT.Abs,
-                                 bias=cols[:, j : j + 1], scale=-1.0)
-            dist.append(d)
+            qw, qs = q_mx[j]
+            a = psum.tile([P, N], F32, name=f"a{j}", tag=score_tags[j])
+            nc.tensor.matmul_mx(out=a[:], lhsT=qw[:].bitcast(FP8X4), lhsT_scale=qs[:],
+                                rhs=kw_g[:].bitcast(FP8X4), rhs_scale=ks_plane[:], start=True, stop=True)
+            scores.append(a)
 
         acc = []
         for j in range(NB):
             o = psum.tile([P, PACK, QB], F32, name=f"acc{j}", tag=f"o{j}")
-            ls_col = cols[:, 2 * NB + j : 2 * NB + j + 1].to_broadcast([P, P])
+            ls_col = cols[:, j : j + 1].to_broadcast([P, P])
             for r in range(PACK):
                 nc.tensor.matmul(o[:, r, :], ls_col, ident[:], is_transpose=True, start=(r == 0), stop=False)
             acc.append(o)
@@ -114,29 +132,31 @@ def tile_attend_plw_alibi_topk_kernel(tc, qT, k_words, k_scales, ps, sl, pq, ls,
         y_scales = sb.tile([P, NQ], U8, name="y_scales", align_bytes=64)
         out_rows = out_0.rearrange("(s r) q -> s r q", r=PACK)
         out_words = out_1[0].rearrange("p q u -> p (q u)").bitcast(I32)
-        score_tags = ("f0", "f3", "f1", "f2")
 
+        ys = []
         for j in range(NB):
             cs = slice(j * QB, (j + 1) * QB)
-            qw, qs = q_mx[j]
-            a = psum.tile([P, N], F32, name=f"a{j}", tag=score_tags[j])
-            nc.tensor.matmul_mx(out=a[:], lhsT=qw[:].bitcast(FP8X4), lhsT_scale=qs[:],
-                                rhs=kw_g[:].bitcast(FP8X4), rhs_scale=ks_plane[:], start=True, stop=True)
             z = sb.tile([P, PACK, P], F32, name=f"z{j}")
-            nc.vector.scalar_tensor_tensor(z[:], dist[j][:], cols[:, NB + j : NB + j + 1],
-                                           a[:].rearrange("q (s r) -> q r s", r=PACK), ALU.mult, ALU.subtract)
+            nc.vector.scalar_tensor_tensor(z[:], dist[j][:], cols[:, 2 * NB + j : 2 * NB + j + 1],
+                                           scores[j][:].rearrange("q (s r) -> q r s", r=PACK), ALU.mult, ALU.subtract)
             for r in range(PACK):
                 nc.tensor.matmul(acc[j][:, r, :], z[:, r, :], ident[:], is_transpose=True, start=False,
                                  stop=(r == PACK - 1))
             y = sb.tile([P, PACK, QB], F32, name=f"y{j}")
             nc.scalar.activation(y[:], acc[j][:], ACT.Exp, scale=-1.0)
             nc.sync.dma_start(out_rows[:, :, cs], y[:])
-            yb = sb.tile([P, QB, PACK], BF16, name=f"yb{j}", align_bytes=64)
+            ys.append(y)
+        for j in range(NB):
+            cs = slice(j * QB, (j + 1) * QB)
+            yb = late.tile([P, QB, PACK], BF16, name=f"yb{j}", offset=AT_DIST + 4 * N * (NB - 1) + 2 * N * j,
+                           align_bytes=64)
             nc.vector.tensor_copy(yb[:].rearrange("p (c i) t -> p c t i", i=4),
-                                  y[:].rearrange("p t (c i) -> p c t i", i=4))
+                                  ys[j][:].rearrange("p t (c i) -> p c t i", i=4))
             nc.vector.quantize_mx(out=y_words[:, cs].bitcast(FP8X4), scales=y_scales[:, cs],
                                   in_=yb[:].rearrange("p c t -> p (c t)"))
-            nc.sync.dma_start(out_words[:, cs], y_words[:, cs].bitcast(I32))
+            if j % 2:
+                hs = slice((j - 1) * QB, (j + 1) * QB)
+                nc.sync.dma_start(out_words[:, hs], y_words[:, hs].bitcast(I32))
         for quad in range(4):
             eng = nc.scalar if quad % 2 else nc.sync
             eng.dma_start(out_2[0, 4 * quad : 4 * quad + 4, :].bitcast(I32),

@@ -95,8 +95,8 @@ def tile_attend_plw_alibi_topk_kernel(tc, qT, k_words, k_scales, ps, sl, pq, ls,
 
         dist = []
         for j in range(NB):
-            d = late.tile([P, PACK, P], F32, name=f"dist{j}", offset=AT_DIST + 4 * N * j, align_bytes=64)
-            nc.scalar.activation(d[:], ps_bc[:].rearrange("q (s r) -> q r s", r=PACK), ACT.Abs,
+            d = late.tile([P, 2, P, 2], F32, name=f"dist{j}", offset=AT_DIST + 4 * N * j, align_bytes=64)
+            nc.scalar.activation(d[:], ps_bc[:].rearrange("q (s h e) -> q h s e", h=2, e=2), ACT.Abs,
                                  bias=cols[:, NB + j : NB + j + 1], scale=-1.0)
             dist.append(d)
 
@@ -136,12 +136,14 @@ def tile_attend_plw_alibi_topk_kernel(tc, qT, k_words, k_scales, ps, sl, pq, ls,
         ys = []
         for j in range(NB):
             cs = slice(j * QB, (j + 1) * QB)
-            z = sb.tile([P, PACK, P], F32, name=f"z{j}")
-            nc.vector.scalar_tensor_tensor(z[:], dist[j][:], cols[:, 2 * NB + j : 2 * NB + j + 1],
-                                           scores[j][:].rearrange("q (s r) -> q r s", r=PACK), ALU.mult, ALU.subtract)
-            for r in range(PACK):
-                nc.tensor.matmul(acc[j][:, r, :], z[:, r, :], ident[:], is_transpose=True, start=False,
-                                 stop=(r == PACK - 1))
+            pairs = scores[j][:].rearrange("q (s h e) -> q h s e", h=2, e=2)
+            for h in range(2):
+                z = sb.tile([P, P, 2], F32, name=f"z{j}_{h}")
+                nc.vector.scalar_tensor_tensor(z[:], dist[j][:, h], cols[:, 2 * NB + j : 2 * NB + j + 1],
+                                               pairs[:, h], ALU.mult, ALU.subtract)
+                for e in range(2):
+                    nc.tensor.matmul(acc[j][:, 2 * h + e, :], z[:, :, e], ident[:], is_transpose=True, start=False,
+                                     stop=(2 * h + e == PACK - 1))
             y = sb.tile([P, PACK, QB], F32, name=f"y{j}")
             nc.scalar.activation(y[:], acc[j][:], ACT.Exp, scale=-1.0)
             nc.sync.dma_start(out_rows[:, :, cs], y[:])

@@ -28,7 +28,7 @@ def tile_attend_plw_alibi_topk_kernel(tc, qT, k_words, k_scales, ps, sl, pq, ls,
         late = ctx.enter_context(tc.tile_pool(name="late", bufs=1))
         psum = ctx.enter_context(tc.psum_pool(name="psum", bufs=1))
 
-        AT_KS, AT_PS, AT_KW, AT_DIST = 0, 2 * T, 6 * T, 10 * T
+        AT_KS, AT_PS, AT_KW, AT_DIST, AT_PEN = 0, 2 * T, 6 * T, 10 * T, 14 * T
         offsets = sb.tile([P, N // 16], U16, name="offsets")
         ks_win = late.tile([P, T], U8, name="ks_win", offset=AT_KS, align_bytes=64)
         ps_win = late.tile([P, T], F32, name="ps_win", offset=AT_PS)
@@ -40,8 +40,10 @@ def tile_attend_plw_alibi_topk_kernel(tc, qT, k_words, k_scales, ps, sl, pq, ls,
         q_src = qT[0].rearrange("(p j) w -> p j w", j=PACK)
         q_raw = [sb.tile([P, PACK, HALF], F32, name="q_raw0")]
         KS0 = 48
-        ROW0 = P - 3 * NB
+        NROW = 3 * NB
+        ROW0 = P - NROW
         CUT = 3 * T // 4
+        SPREAD = 2
 
         nc.sync.dma_start(offsets[:], offs)
         nc.sync.dma_start(ks_win[:].bitcast(I32)[KS0 : KS0 + 16, :], k_scales[0].bitcast(I32))
@@ -55,21 +57,17 @@ def tile_attend_plw_alibi_topk_kernel(tc, qT, k_words, k_scales, ps, sl, pq, ls,
         nc.vector.memset(ks_win[:].bitcast(I32)[0:KS0, :], 0)
         nc.vector.memset(ps_win[0 : P - 1, 0:CUT], 0.0)
         nc.gpsimd.memset(rows[0:ROW0, :], 0.0)
+        nc.gpsimd.memset(ks_win[:].bitcast(I32)[64:P, :], 0)
+        nc.gpsimd.memset(ps_win[0 : P - 1, CUT:T], 0.0)
         nc.gpsimd.memset(ident[:], 0.0)
         nc.gpsimd.affine_select(out=ident[:], in_=ident[:], compare_op=ALU.not_equal, fill=1.0, base=0,
                                 pattern=[[-1, P]], channel_multiplier=1)
-        nc.gpsimd.memset(ks_win[:].bitcast(I32)[64:P, :], 0)
-        nc.gpsimd.memset(ps_win[0 : P - 1, CUT:T], 0.0)
         nc.gpsimd.memset(ks_plane[:].bitcast(I32), 0)
         nc.scalar.activation(warm[0:64, :], rows[0:64, 0:8], ACT.Exp)
 
-        rows_t = psum.tile([P, N], F32, name="rows_t", tag="b0")
-        nc.tensor.transpose(rows_t[:, 0:P], rows[:], ident[:])
-        cols = sb.tile([P, 3 * NB], F32, name="cols")
-        nc.vector.tensor_copy(cols[:], rows_t[:, ROW0:P])
-
-        ps_g = sb.tile([P, N], F32, name="ps_g")
-        nc.scalar.activation(ps_g[:], ps_win[:].indirect(offsets[:]), ACT.Copy)
+        ps_g = [sb.tile([P, N // 2], F32, name=f"ps_g{h}") for h in range(2)]
+        for h in range(2):
+            nc.scalar.activation(ps_g[h][:], ps_win[:].indirect(offsets[:, h * N // 32 : (h + 1) * N // 32]), ACT.Copy)
         ks_g = sb.tile([P, N], U8, name="ks_g", align_bytes=64)
         nc.vector.tensor_copy(ks_g[:], ks_win[:].indirect(offsets[:]))
         for quad in range(4):
@@ -80,18 +78,22 @@ def tile_attend_plw_alibi_topk_kernel(tc, qT, k_words, k_scales, ps, sl, pq, ls,
         kw_g = late.tile([P, N], U32, name="kw_g", offset=AT_PS, align_bytes=64)
         nc.vector.tensor_copy(kw_g[:], kw_win[:].bitcast(U32).indirect(offsets[:]))
 
-        ps_col = []
-        for h in range(2):
-            ps_t = psum.tile([P, 2, P], F32, name=f"ps_t{h}", tag=f"o{2 + h}")
-            for c in range(2):
-                nc.tensor.transpose(ps_t[:, c, :], ps_g[:, (2 * h + c) * P : (2 * h + c + 1) * P], ident[:])
-            col = sb.tile([P, 2], F32, name=f"ps_col{h}")
-            nc.scalar.copy(col[:], ps_t[:, :, P - 1])
-            ps_col.append(col)
-        ps_bc = psum.tile([P, N], F32, name="ps_bc", tag="b2")
+        turned = psum.tile([P, 2, P], F32, name="turned", tag="b0")
+        for c in range(2):
+            nc.tensor.transpose(turned[:, c, :], ps_g[0][:, c * P : (c + 1) * P], ident[:])
+        head = sb.tile([P, 2], F32, name="head")
+        nc.scalar.copy(head[:], turned[:, :, P - 1])
+        turned2 = psum.tile([P, 3, P], F32, name="turned2", tag="b1")
+        nc.tensor.transpose(turned2[:, 2, :], rows[:], ident[:])
+        for c in range(2):
+            nc.tensor.transpose(turned2[:, c, :], ps_g[1][:, c * P : (c + 1) * P], ident[:])
+        rest = sb.tile([P, 3, NROW], F32, name="rest")
+        nc.scalar.copy(rest[:], turned2[:, :, ROW0:P])
+        cols = rest[:, 2, :]
+        ps_col = [head[:, 0:1], head[:, 1:2], rest[:, 0, NROW - 1 : NROW], rest[:, 1, NROW - 1 : NROW]]
+        ps_bc = psum.tile([P, N], F32, name="ps_bc", tag="o3")
         for c in range(N // P):
-            nc.tensor.transpose(ps_bc[:, c * P : (c + 1) * P],
-                                ps_col[c // 2][:, c % 2 : c % 2 + 1].to_broadcast([P, P]), ident[:])
+            nc.tensor.transpose(ps_bc[:, c * P : (c + 1) * P], ps_col[c].to_broadcast([P, P]), ident[:])
 
         dist = []
         for j in range(NB):
@@ -111,7 +113,7 @@ def tile_attend_plw_alibi_topk_kernel(tc, qT, k_words, k_scales, ps, sl, pq, ls,
             nc.vector.quantize_mx(out=qw[:].bitcast(FP8X4), scales=qs[:], in_=qb[:].rearrange("p c t -> p (c t)"))
             q_mx.append((qw, qs))
 
-        score_tags = ("b3", "b1", "b0", "b2")
+        score_tags = ("b2", "b3", "b0", "b1")
         scores = []
         for j in range(NB):
             qw, qs = q_mx[j]
@@ -121,37 +123,49 @@ def tile_attend_plw_alibi_topk_kernel(tc, qT, k_words, k_scales, ps, sl, pq, ls,
             scores.append(a)
 
         acc = []
-        for j in range(NB):
+        for j in range(SPREAD):
             o = psum.tile([P, PACK, QB], F32, name=f"acc{j}", tag=f"o{j}")
             ls_col = cols[:, j : j + 1].to_broadcast([P, P])
             for r in range(PACK):
                 nc.tensor.matmul(o[:, r, :], ls_col, ident[:], is_transpose=True, start=(r == 0), stop=False)
             acc.append(o)
+        pen = {}
+        for j in range(SPREAD, NB):
+            pen[j] = late.tile([P, 2, P, 2], F32, name=f"pen{j}", offset=AT_PEN + 4 * N * (j - SPREAD), align_bytes=64)
+            nc.scalar.activation(pen[j][:], dist[j][:], ACT.Identity, bias=cols[:, j : j + 1],
+                                 scale=cols[:, 2 * NB + j : 2 * NB + j + 1])
 
         y_words = sb.tile([P, NQ], U32, name="y_words", align_bytes=64)
         y_scales = sb.tile([P, NQ], U8, name="y_scales", align_bytes=64)
         out_rows = out_0.rearrange("(s r) q -> s r q", r=PACK)
         out_words = out_1[0].rearrange("p q u -> p (q u)").bitcast(I32)
 
+        AT_Z = (AT_KS, AT_KW + 2 * T)
         ys = []
         for j in range(NB):
             cs = slice(j * QB, (j + 1) * QB)
             pairs = scores[j][:].rearrange("q (s h e) -> q h s e", h=2, e=2)
+            if j >= SPREAD:
+                acc.append(psum.tile([P, PACK, QB], F32, name=f"acc{j}", tag=f"o{j}"))
             for h in range(2):
-                z = sb.tile([P, P, 2], F32, name=f"z{j}_{h}")
-                nc.vector.scalar_tensor_tensor(z[:], dist[j][:, h], cols[:, 2 * NB + j : 2 * NB + j + 1],
-                                               pairs[:, h], ALU.mult, ALU.subtract)
+                z = late.tile([P, P, 2], F32, name=f"z{j}_{h}", offset=AT_Z[j // 2] + 2 * N * (2 * (j % 2) + h))
+                if j < SPREAD:
+                    nc.vector.scalar_tensor_tensor(z[:], dist[j][:, h], cols[:, 2 * NB + j : 2 * NB + j + 1],
+                                                   pairs[:, h], ALU.mult, ALU.subtract)
+                else:
+                    nc.vector.tensor_tensor(z[:], pen[j][:, h], pairs[:, h], ALU.subtract)
                 for e in range(2):
-                    nc.tensor.matmul(acc[j][:, 2 * h + e, :], z[:, :, e], ident[:], is_transpose=True, start=False,
-                                     stop=(2 * h + e == PACK - 1))
+                    r = 2 * h + e
+                    nc.tensor.matmul(acc[j][:, r, :], z[:, :, e], ident[:], is_transpose=True,
+                                     start=(j >= SPREAD and r == 0), stop=(r == PACK - 1))
             y = sb.tile([P, PACK, QB], F32, name=f"y{j}")
             nc.scalar.activation(y[:], acc[j][:], ACT.Exp, scale=-1.0)
             nc.sync.dma_start(out_rows[:, :, cs], y[:])
             ys.append(y)
         for j in range(NB):
             cs = slice(j * QB, (j + 1) * QB)
-            yb = late.tile([P, QB, PACK], BF16, name=f"yb{j}", offset=AT_DIST + 4 * N * (NB - 1) + 2 * N * j,
-                           align_bytes=64)
+            yb = late.tile([P, QB, PACK], BF16, name=f"yb{j}",
+                           offset=AT_PEN + 4 * N * (NB - 1 - SPREAD) + 2 * N * j, align_bytes=64)
             nc.vector.tensor_copy(yb[:].rearrange("p (c i) t -> p c t i", i=4),
                                   ys[j][:].rearrange("p t (c i) -> p c t i", i=4))
             nc.vector.quantize_mx(out=y_words[:, cs].bitcast(FP8X4), scales=y_scales[:, cs],

@@ -43,7 +43,6 @@ def tile_attend_plw_alibi_topk_kernel(tc, qT, k_words, k_scales, ps, sl, pq, ls,
         NROW = 3 * NB
         ROW0 = P - NROW
         CUT = 3 * T // 4
-        SPREAD = 2
 
         nc.sync.dma_start(offsets[:], offs)
         nc.sync.dma_start(ks_win[:].bitcast(I32)[KS0 : KS0 + 16, :], k_scales[0].bitcast(I32))
@@ -122,16 +121,16 @@ def tile_attend_plw_alibi_topk_kernel(tc, qT, k_words, k_scales, ps, sl, pq, ls,
                                 rhs=kw_g[:].bitcast(FP8X4), rhs_scale=ks_plane[:], start=True, stop=True)
             scores.append(a)
 
-        acc = []
-        for j in range(SPREAD):
-            o = psum.tile([P, PACK, QB], F32, name=f"acc{j}", tag=f"o{j}")
-            ls_col = cols[:, j : j + 1].to_broadcast([P, P])
-            for r in range(PACK):
-                nc.tensor.matmul(o[:, r, :], ls_col, ident[:], is_transpose=True, start=(r == 0), stop=False)
-            acc.append(o)
+        acc_early = [psum.tile([P, 2, HALF], F32, name=f"acc_early{h}", tag=f"o{h}") for h in range(2)]
+        for h in range(2):
+            for j in range(2):
+                ls_col = cols[:, j : j + 1].to_broadcast([P, P])
+                for e in range(2):
+                    nc.tensor.matmul(acc_early[h][:, e, j * QB : (j + 1) * QB], ls_col, ident[:], is_transpose=True,
+                                     start=(j == 0 and e == 0), stop=False)
         pen = {}
-        for j in range(SPREAD, NB):
-            pen[j] = late.tile([P, 2, P, 2], F32, name=f"pen{j}", offset=AT_PEN + 4 * N * (j - SPREAD), align_bytes=64)
+        for j in range(2, NB):
+            pen[j] = late.tile([P, 2, P, 2], F32, name=f"pen{j}", offset=AT_PEN + 4 * N * (j - 2), align_bytes=64)
             nc.scalar.activation(pen[j][:], dist[j][:], ACT.Identity, bias=cols[:, j : j + 1],
                                  scale=cols[:, 2 * NB + j : 2 * NB + j + 1])
 
@@ -139,40 +138,39 @@ def tile_attend_plw_alibi_topk_kernel(tc, qT, k_words, k_scales, ps, sl, pq, ls,
         y_scales = sb.tile([P, NQ], U8, name="y_scales", align_bytes=64)
         out_rows = out_0.rearrange("(s r) q -> s r q", r=PACK)
         out_words = out_1[0].rearrange("p q u -> p (q u)").bitcast(I32)
+        y = [sb.tile([P, PACK, HALF], F32, name=f"y{g}") for g in range(2)]
+        pairs = [a[:].rearrange("q (s h e) -> q h s e", h=2, e=2) for a in scores]
 
-        AT_Z = (AT_KS, AT_KW + 2 * T)
-        ys = []
-        for j in range(NB):
-            cs = slice(j * QB, (j + 1) * QB)
-            pairs = scores[j][:].rearrange("q (s h e) -> q h s e", h=2, e=2)
-            if j >= SPREAD:
-                acc.append(psum.tile([P, PACK, QB], F32, name=f"acc{j}", tag=f"o{j}"))
-            for h in range(2):
-                z = late.tile([P, P, 2], F32, name=f"z{j}_{h}", offset=AT_Z[j // 2] + 2 * N * (2 * (j % 2) + h))
-                if j < SPREAD:
-                    nc.vector.scalar_tensor_tensor(z[:], dist[j][:, h], cols[:, 2 * NB + j : 2 * NB + j + 1],
-                                                   pairs[:, h], ALU.mult, ALU.subtract)
-                else:
-                    nc.vector.tensor_tensor(z[:], pen[j][:, h], pairs[:, h], ALU.subtract)
+        for h in range(2):
+            for j in range(2):
+                z = late.tile([P, P, 2], F32, name=f"z{j}_{h}", offset=AT_KS + 2 * N * (2 * h + j))
+                nc.vector.scalar_tensor_tensor(z[:], dist[j][:, h], cols[:, 2 * NB + j : 2 * NB + j + 1],
+                                               pairs[j][:, h], ALU.mult, ALU.subtract)
                 for e in range(2):
-                    r = 2 * h + e
-                    nc.tensor.matmul(acc[j][:, r, :], z[:, :, e], ident[:], is_transpose=True,
-                                     start=(j >= SPREAD and r == 0), stop=(r == PACK - 1))
-            y = sb.tile([P, PACK, QB], F32, name=f"y{j}")
-            nc.scalar.activation(y[:], acc[j][:], ACT.Exp, scale=-1.0)
-            nc.sync.dma_start(out_rows[:, :, cs], y[:])
-            ys.append(y)
+                    nc.tensor.matmul(acc_early[h][:, e, j * QB : (j + 1) * QB], z[:, :, e], ident[:],
+                                     is_transpose=True, start=False, stop=(j == 1 and e == 1))
+            nc.scalar.activation(y[0][:, 2 * h : 2 * h + 2, :], acc_early[h][:], ACT.Exp, scale=-1.0)
+            nc.sync.dma_start(out_rows[:, 2 * h : 2 * h + 2, 0:HALF], y[0][:, 2 * h : 2 * h + 2, :])
+        for j in range(2, NB):
+            acc = psum.tile([P, PACK, QB], F32, name=f"acc{j}", tag=f"o{j}")
+            for h in range(2):
+                z = sb.tile([P, P, 2], F32, name=f"z{j}_{h}")
+                nc.vector.tensor_tensor(z[:], pen[j][:, h], pairs[j][:, h], ALU.subtract)
+                for e in range(2):
+                    nc.tensor.transpose(acc[:, 2 * h + e, :], z[:, :, e], ident[:])
+            nc.scalar.activation(y[1][:, :, (j - 2) * QB : (j - 1) * QB], acc[:], ACT.Exp, scale=-1.0)
+        nc.sync.dma_start(out_rows[:, :, HALF:NQ], y[1][:])
         for j in range(NB):
             cs = slice(j * QB, (j + 1) * QB)
-            yb = late.tile([P, QB, PACK], BF16, name=f"yb{j}",
-                           offset=AT_PEN + 4 * N * (NB - 1 - SPREAD) + 2 * N * j, align_bytes=64)
+            g, c0 = divmod(j * QB, HALF)
+            yb = late.tile([P, QB, PACK], BF16, name=f"yb{j}", offset=AT_PEN + 4 * N + 2 * N * j, align_bytes=64)
             nc.vector.tensor_copy(yb[:].rearrange("p (c i) t -> p c t i", i=4),
-                                  ys[j][:].rearrange("p t (c i) -> p c t i", i=4))
+                                  y[g][:, :, c0 : c0 + QB].rearrange("p t (c i) -> p c t i", i=4))
             nc.vector.quantize_mx(out=y_words[:, cs].bitcast(FP8X4), scales=y_scales[:, cs],
                                   in_=yb[:].rearrange("p c t -> p (c t)"))
             if j % 2:
                 hs = slice((j - 1) * QB, (j + 1) * QB)
-                nc.sync.dma_start(out_words[:, hs], y_words[:, hs].bitcast(I32))
+                (nc.scalar if j == NB - 1 else nc.sync).dma_start(out_words[:, hs], y_words[:, hs].bitcast(I32))
         for quad in range(4):
             eng = nc.scalar if quad % 2 else nc.sync
             eng.dma_start(out_2[0, 4 * quad : 4 * quad + 4, :].bitcast(I32),

@@ -143,21 +143,21 @@ def tile_attend_plw_alibi_topk_kernel(tc, qT, k_words, k_scales, ps, sl, pq, ls,
 
         for h in range(2):
             for j in range(2):
-                z = late.tile([P, P, 2], F32, name=f"z{j}_{h}", offset=AT_KS + 2 * N * (2 * h + j))
-                nc.vector.scalar_tensor_tensor(z[:], dist[j][:, h], cols[:, 2 * NB + j : 2 * NB + j + 1],
+                z = late.tile([P, 2, P], F32, name=f"z{j}_{h}", offset=AT_KS + 2 * N * (2 * h + j))
+                nc.vector.scalar_tensor_tensor(z[:].rearrange("q e s -> q s e"), dist[j][:, h], cols[:, 2 * NB + j : 2 * NB + j + 1],
                                                pairs[j][:, h], ALU.mult, ALU.subtract)
                 for e in range(2):
-                    nc.tensor.matmul(acc_early[h][:, e, j * QB : (j + 1) * QB], z[:, :, e], ident[:],
+                    nc.tensor.matmul(acc_early[h][:, e, j * QB : (j + 1) * QB], z[:, e, :], ident[:],
                                      is_transpose=True, start=False, stop=(j == 1 and e == 1))
             nc.scalar.activation(y[0][:, 2 * h : 2 * h + 2, :], acc_early[h][:], ACT.Exp, scale=-1.0)
             nc.sync.dma_start(out_rows[:, 2 * h : 2 * h + 2, 0:HALF], y[0][:, 2 * h : 2 * h + 2, :])
         for j in range(2, NB):
             acc = psum.tile([P, PACK, QB], F32, name=f"acc{j}", tag=f"o{j}")
             for h in range(2):
-                z = sb.tile([P, P, 2], F32, name=f"z{j}_{h}")
-                nc.vector.tensor_tensor(z[:], pen[j][:, h], pairs[j][:, h], ALU.subtract)
+                z = sb.tile([P, 2, P], F32, name=f"z{j}_{h}")
+                nc.vector.tensor_tensor(z[:].rearrange("q e s -> q s e"), pen[j][:, h], pairs[j][:, h], ALU.subtract)
                 for e in range(2):
-                    nc.tensor.transpose(acc[:, 2 * h + e, :], z[:, :, e], ident[:])
+                    nc.tensor.transpose(acc[:, 2 * h + e, :], z[:, e, :], ident[:])
             nc.scalar.activation(y[1][:, :, (j - 2) * QB : (j - 1) * QB], acc[:], ACT.Exp, scale=-1.0)
         nc.sync.dma_start(out_rows[:, :, HALF:NQ], y[1][:])
         for j in range(NB):

@@ -28,7 +28,8 @@ def tile_attend_plw_alibi_topk_kernel(tc, qT, k_words, k_scales, ps, sl, pq, ls,
         late = ctx.enter_context(tc.tile_pool(name="late", bufs=1))
         psum = ctx.enter_context(tc.psum_pool(name="psum", bufs=1))
 
-        AT_KS, AT_PS, AT_KW, AT_DIST, AT_PEN = 0, 2 * T, 6 * T, 10 * T, 14 * T
+        KB = 1024
+        AT_KS, AT_PS, AT_KW, AT_PEN = 2 * KB, 6 * KB, 14 * KB, 22 * KB
         offsets = sb.tile([P, N // 16], U16, name="offsets")
         ks_win = late.tile([P, T], U8, name="ks_win", offset=AT_KS, align_bytes=64)
         ps_win = late.tile([P, T], F32, name="ps_win", offset=AT_PS)
@@ -38,11 +39,12 @@ def tile_attend_plw_alibi_topk_kernel(tc, qT, k_words, k_scales, ps, sl, pq, ls,
         warm = sb.tile([P, 8], F32, name="warm")
         ks_plane = sb.tile([P, N], U8, name="ks_plane", align_bytes=64)
         q_src = qT[0].rearrange("(p j) w -> p j w", j=PACK)
-        q_raw = [sb.tile([P, PACK, HALF], F32, name="q_raw0")]
+        q_first = sb.tile([P, PACK, HALF], F32, name="q_first")
         KS0 = 48
         NROW = 3 * NB
         ROW0 = P - NROW
         CUT = 3 * T // 4
+        NH = N // 2
 
         nc.sync.dma_start(offsets[:], offs)
         nc.sync.dma_start(ks_win[:].bitcast(I32)[KS0 : KS0 + 16, :], k_scales[0].bitcast(I32))
@@ -51,7 +53,7 @@ def tile_attend_plw_alibi_topk_kernel(tc, qT, k_words, k_scales, ps, sl, pq, ls,
             nc.scalar.dma_start(rows[ROW0 + NB * i : ROW0 + NB * (i + 1), :],
                                 vec[0].rearrange("o (c m) -> (o c) m", m=QB))
         nc.sync.dma_start(kw_win[:], k_words[0].rearrange("p t r -> p (t r)").bitcast(I32))
-        nc.sync.dma_start(q_raw[0][:], q_src[:, :, 0:HALF])
+        nc.sync.dma_start(q_first[:], q_src[:, :, 0:HALF])
 
         nc.vector.memset(ks_win[:].bitcast(I32)[0:KS0, :], 0)
         nc.vector.memset(ps_win[0 : P - 1, 0:CUT], 0.0)
@@ -64,16 +66,18 @@ def tile_attend_plw_alibi_topk_kernel(tc, qT, k_words, k_scales, ps, sl, pq, ls,
         nc.gpsimd.memset(ks_plane[:].bitcast(I32), 0)
         nc.scalar.activation(warm[0:64, :], rows[0:64, 0:8], ACT.Exp)
 
-        ps_g = [sb.tile([P, N // 2], F32, name=f"ps_g{h}") for h in range(2)]
+        ps_g = [sb.tile([P, NH], F32, name=f"ps_g{h}") for h in range(2)]
         for h in range(2):
-            nc.scalar.activation(ps_g[h][:], ps_win[:].indirect(offsets[:, h * N // 32 : (h + 1) * N // 32]), ACT.Copy)
+            nc.scalar.activation(ps_g[h][:], ps_win[:].indirect(offsets[:, h * NH // 16 : (h + 1) * NH // 16]), ACT.Copy)
         ks_g = sb.tile([P, N], U8, name="ks_g", align_bytes=64)
         nc.vector.tensor_copy(ks_g[:], ks_win[:].indirect(offsets[:]))
         for quad in range(4):
             nc.sync.dma_start(ks_plane[:].bitcast(I32)[32 * quad : 32 * quad + 4, :],
                               ks_g[:].bitcast(I32)[KS0 + 4 * quad : KS0 + 4 * quad + 4, :])
-        q_raw.append(late.tile([P, PACK, HALF], F32, name="q_raw1", offset=AT_KS))
-        nc.sync.dma_start(q_raw[1][:], q_src[:, :, HALF:NQ])
+        q_late = late.tile([P, PACK, HALF], F32, name="q_late", offset=0)
+        nc.sync.dma_start(q_late[:], q_src[:, :, HALF:NQ])
+        q_blocks = [t[:, :, c0 : c0 + QB] for t in (q_first, q_late) for c0 in (0, QB)]
+        at_z = (0, KB, 2 * KB, 3 * KB)
         kw_g = late.tile([P, N], U32, name="kw_g", offset=AT_PS, align_bytes=64)
         nc.vector.tensor_copy(kw_g[:], kw_win[:].bitcast(U32).indirect(offsets[:]))
 
@@ -96,41 +100,40 @@ def tile_attend_plw_alibi_topk_kernel(tc, qT, k_words, k_scales, ps, sl, pq, ls,
 
         dist = []
         for j in range(NB):
-            d = late.tile([P, 2, P, 2], F32, name=f"dist{j}", offset=AT_DIST + 4 * N * j, align_bytes=64)
+            d = sb.tile([P, 2, P, 2], F32, name=f"dist{j}")
             nc.scalar.activation(d[:], ps_bc[:].rearrange("q (s h e) -> q h s e", h=2, e=2), ACT.Abs,
                                  bias=cols[:, NB + j : NB + j + 1], scale=-1.0)
             dist.append(d)
 
         q_mx = []
         for j in range(NB):
-            h, c0 = divmod(j * QB, HALF)
-            qb = late.tile([P, QB, PACK], BF16, name=f"qb{j}", offset=AT_KW + 2 * N * j, align_bytes=64)
+            qb = late.tile([P, QB, PACK], BF16, name=f"qb{j}", offset=AT_KW + KB * j, align_bytes=64)
             nc.vector.tensor_copy(qb[:].rearrange("p (c i) t -> p c t i", i=4),
-                                  q_raw[h][:, :, c0 : c0 + QB].rearrange("p t (c i) -> p c t i", i=4))
+                                  q_blocks[j].rearrange("p t (c i) -> p c t i", i=4))
             qw = sb.tile([P, QB], U32, name=f"qw{j}", align_bytes=64)
             qs = sb.tile([P, QB], U8, name=f"qs{j}", align_bytes=64)
             nc.vector.quantize_mx(out=qw[:].bitcast(FP8X4), scales=qs[:], in_=qb[:].rearrange("p c t -> p (c t)"))
             q_mx.append((qw, qs))
 
         score_tags = ("b2", "b3", "b0", "b1")
-        scores = []
+        pairs = []
         for j in range(NB):
             qw, qs = q_mx[j]
             a = psum.tile([P, N], F32, name=f"a{j}", tag=score_tags[j])
             nc.tensor.matmul_mx(out=a[:], lhsT=qw[:].bitcast(FP8X4), lhsT_scale=qs[:],
                                 rhs=kw_g[:].bitcast(FP8X4), rhs_scale=ks_plane[:], start=True, stop=True)
-            scores.append(a)
+            pairs.append(a[:].rearrange("q (s h e) -> q h s e", h=2, e=2))
 
-        acc_early = [psum.tile([P, 2, HALF], F32, name=f"acc_early{h}", tag=f"o{h}") for h in range(2)]
+        acc = {(0, h): psum.tile([P, 2, HALF], F32, name=f"acc0_{h}", tag=f"o{h}") for h in range(2)}
         for h in range(2):
             for j in range(2):
                 ls_col = cols[:, j : j + 1].to_broadcast([P, P])
                 for e in range(2):
-                    nc.tensor.matmul(acc_early[h][:, e, j * QB : (j + 1) * QB], ls_col, ident[:], is_transpose=True,
+                    nc.tensor.matmul(acc[0, h][:, e, j * QB : (j + 1) * QB], ls_col, ident[:], is_transpose=True,
                                      start=(j == 0 and e == 0), stop=False)
         pen = {}
         for j in range(2, NB):
-            pen[j] = late.tile([P, 2, P, 2], F32, name=f"pen{j}", offset=AT_PEN + 4 * N * (j - 2), align_bytes=64)
+            pen[j] = late.tile([P, 2, P, 2], F32, name=f"pen{j}", offset=AT_PEN + 2 * KB * (j - 2), align_bytes=64)
             nc.scalar.activation(pen[j][:], dist[j][:], ACT.Identity, bias=cols[:, j : j + 1],
                                  scale=cols[:, 2 * NB + j : 2 * NB + j + 1])
 
@@ -138,39 +141,40 @@ def tile_attend_plw_alibi_topk_kernel(tc, qT, k_words, k_scales, ps, sl, pq, ls,
         y_scales = sb.tile([P, NQ], U8, name="y_scales", align_bytes=64)
         out_rows = out_0.rearrange("(s r) q -> s r q", r=PACK)
         out_words = out_1[0].rearrange("p q u -> p (q u)").bitcast(I32)
+
         y = [sb.tile([P, PACK, HALF], F32, name=f"y{g}") for g in range(2)]
-        pairs = [a[:].rearrange("q (s h e) -> q h s e", h=2, e=2) for a in scores]
 
         for h in range(2):
             for j in range(2):
-                z = late.tile([P, 2, P], F32, name=f"z{j}_{h}", offset=AT_KS + 2 * N * (2 * h + j))
-                nc.vector.scalar_tensor_tensor(z[:].rearrange("q e s -> q s e"), dist[j][:, h], cols[:, 2 * NB + j : 2 * NB + j + 1],
-                                               pairs[j][:, h], ALU.mult, ALU.subtract)
+                z = late.tile([P, 2, P], F32, name=f"z{j}_{h}", offset=at_z[2 * h + j])
+                nc.vector.scalar_tensor_tensor(z[:].rearrange("q e s -> q s e"), dist[j][:, h],
+                                               cols[:, 2 * NB + j : 2 * NB + j + 1], pairs[j][:, h],
+                                               ALU.mult, ALU.subtract)
                 for e in range(2):
-                    nc.tensor.matmul(acc_early[h][:, e, j * QB : (j + 1) * QB], z[:, e, :], ident[:],
+                    nc.tensor.matmul(acc[0, h][:, e, j * QB : (j + 1) * QB], z[:, e, :], ident[:],
                                      is_transpose=True, start=False, stop=(j == 1 and e == 1))
-            nc.scalar.activation(y[0][:, 2 * h : 2 * h + 2, :], acc_early[h][:], ACT.Exp, scale=-1.0)
+            nc.scalar.activation(y[0][:, 2 * h : 2 * h + 2, :], acc[0, h][:], ACT.Exp, scale=-1.0)
             nc.sync.dma_start(out_rows[:, 2 * h : 2 * h + 2, 0:HALF], y[0][:, 2 * h : 2 * h + 2, :])
         for j in range(2, NB):
-            acc = psum.tile([P, PACK, QB], F32, name=f"acc{j}", tag=f"o{j}")
+            turned_back = psum.tile([P, PACK, QB], F32, name=f"acc{j}", tag=f"o{j}")
             for h in range(2):
                 z = sb.tile([P, 2, P], F32, name=f"z{j}_{h}")
                 nc.vector.tensor_tensor(z[:].rearrange("q e s -> q s e"), pen[j][:, h], pairs[j][:, h], ALU.subtract)
                 for e in range(2):
-                    nc.tensor.transpose(acc[:, 2 * h + e, :], z[:, e, :], ident[:])
-            nc.scalar.activation(y[1][:, :, (j - 2) * QB : (j - 1) * QB], acc[:], ACT.Exp, scale=-1.0)
-        nc.sync.dma_start(out_rows[:, :, HALF:NQ], y[1][:])
+                    nc.tensor.transpose(turned_back[:, 2 * h + e, :], z[:, e, :], ident[:])
+            nc.scalar.activation(y[1][:, :, (j - 2) * QB : (j - 1) * QB], turned_back[:], ACT.Exp, scale=-1.0)
+        nc.scalar.dma_start(out_rows[:, :, HALF:NQ], y[1][:])
         for j in range(NB):
             cs = slice(j * QB, (j + 1) * QB)
             g, c0 = divmod(j * QB, HALF)
-            yb = late.tile([P, QB, PACK], BF16, name=f"yb{j}", offset=AT_PEN + 4 * N + 2 * N * j, align_bytes=64)
+            yb = late.tile([P, QB, PACK], BF16, name=f"yb{j}", offset=AT_PEN + 2 * KB + KB * j, align_bytes=64)
             nc.vector.tensor_copy(yb[:].rearrange("p (c i) t -> p c t i", i=4),
                                   y[g][:, :, c0 : c0 + QB].rearrange("p t (c i) -> p c t i", i=4))
             nc.vector.quantize_mx(out=y_words[:, cs].bitcast(FP8X4), scales=y_scales[:, cs],
                                   in_=yb[:].rearrange("p c t -> p (c t)"))
             if j % 2:
                 hs = slice((j - 1) * QB, (j + 1) * QB)
-                (nc.scalar if j == NB - 1 else nc.sync).dma_start(out_words[:, hs], y_words[:, hs].bitcast(I32))
+                nc.sync.dma_start(out_words[:, hs], y_words[:, hs].bitcast(I32))
         for quad in range(4):
             eng = nc.scalar if quad % 2 else nc.sync
             eng.dma_start(out_2[0, 4 * quad : 4 * quad + 4, :].bitcast(I32),

@@ -133,9 +133,12 @@ def tile_attend_plw_alibi_topk_kernel(tc, qT, k_words, k_scales, ps, sl, pq, ls,
                                      start=(j == 0 and e == 0), stop=False)
         pen = {}
         for j in range(2, NB):
-            pen[j] = late.tile([P, 2, P, 2], F32, name=f"pen{j}", offset=AT_PEN + 2 * KB * (j - 2), align_bytes=64)
-            nc.scalar.activation(pen[j][:], dist[j][:], ACT.Identity, bias=cols[:, j : j + 1],
-                                 scale=cols[:, 2 * NB + j : 2 * NB + j + 1])
+            pen[j] = late.tile([P, 2, P, 2], F32, name=f"pen{j}", offset=AT_PEN if j == 2 else AT_KW + 3 * KB,
+                               align_bytes=64)
+        nc.scalar.activation(pen[2][:], dist[2][:], ACT.Identity, bias=cols[:, 2:3],
+                             scale=cols[:, 2 * NB + 2 : 2 * NB + 3])
+        nc.gpsimd.tensor_scalar(pen[3][:].rearrange("q h s e -> q (h s e)"), dist[3][:].rearrange("q h s e -> q (h s e)"),
+                                cols[:, 2 * NB + 3 : 2 * NB + 4], cols[:, 3:4], ALU.mult, ALU.add)
 
         y_words = sb.tile([P, NQ], U32, name="y_words", align_bytes=64)
         y_scales = sb.tile([P, NQ], U8, name="y_scales", align_bytes=64)
@@ -167,7 +170,7 @@ def tile_attend_plw_alibi_topk_kernel(tc, qT, k_words, k_scales, ps, sl, pq, ls,
         for j in range(NB):
             cs = slice(j * QB, (j + 1) * QB)
             g, c0 = divmod(j * QB, HALF)
-            yb = late.tile([P, QB, PACK], BF16, name=f"yb{j}", offset=AT_PEN + 2 * KB + KB * j, align_bytes=64)
+            yb = late.tile([P, QB, PACK], BF16, name=f"yb{j}", offset=AT_KW + (3 + j) * KB, align_bytes=64)
             nc.vector.tensor_copy(yb[:].rearrange("p (c i) t -> p c t i", i=4),
                                   y[g][:, :, c0 : c0 + QB].rearrange("p t (c i) -> p c t i", i=4))
             nc.vector.quantize_mx(out=y_words[:, cs].bitcast(FP8X4), scales=y_scales[:, cs],

@@ -43,23 +43,23 @@ def tile_attend_plw_alibi_topk_kernel(tc, qT, k_words, k_scales, ps, sl, pq, ls,
         KS0 = 48
         NROW = 3 * NB
         ROW0 = P - NROW
-        CUT = 3 * T // 4
+        CUT = 5 * T // 8
         NH = N // 2
 
         nc.sync.dma_start(offsets[:], offs)
-        nc.sync.dma_start(ks_win[:].bitcast(I32)[KS0 : KS0 + 16, :], k_scales[0].bitcast(I32))
         nc.sync.dma_start(ps_win[P - 1 : P, :], ps[0:1, :])
-        for i, vec in enumerate((ls, pq, sl)):
-            nc.scalar.dma_start(rows[ROW0 + NB * i : ROW0 + NB * (i + 1), :],
-                                vec[0].rearrange("o (c m) -> (o c) m", m=QB))
+        nc.sync.dma_start(ks_win[:].bitcast(I32)[KS0 : KS0 + 16, :], k_scales[0].bitcast(I32))
+        for i, vec, eng in ((1, pq, nc.scalar), (0, ls, nc.scalar), (2, sl, nc.sync)):
+            eng.dma_start(rows[ROW0 + NB * i : ROW0 + NB * (i + 1), :],
+                          vec[0].rearrange("o (c m) -> (o c) m", m=QB))
         nc.sync.dma_start(kw_win[:], k_words[0].rearrange("p t r -> p (t r)").bitcast(I32))
         nc.sync.dma_start(q_first[:], q_src[:, :, 0:HALF])
 
-        nc.vector.memset(ks_win[:].bitcast(I32)[0:KS0, :], 0)
+        nc.vector.memset(rows[0:ROW0, :], 0.0)
         nc.vector.memset(ps_win[0 : P - 1, 0:CUT], 0.0)
-        nc.gpsimd.memset(rows[0:ROW0, :], 0.0)
-        nc.gpsimd.memset(ks_win[:].bitcast(I32)[64:P, :], 0)
+        nc.vector.memset(ks_win[:].bitcast(I32)[0:KS0, :], 0)
         nc.gpsimd.memset(ps_win[0 : P - 1, CUT:T], 0.0)
+        nc.gpsimd.memset(ks_win[:].bitcast(I32)[64:P, :], 0)
         nc.gpsimd.memset(ident[:], 0.0)
         nc.gpsimd.affine_select(out=ident[:], in_=ident[:], compare_op=ALU.not_equal, fill=1.0, base=0,
                                 pattern=[[-1, P]], channel_multiplier=1)
@@ -67,10 +67,11 @@ def tile_attend_plw_alibi_topk_kernel(tc, qT, k_words, k_scales, ps, sl, pq, ls,
         nc.scalar.activation(warm[0:64, :], rows[0:64, 0:8], ACT.Exp)
 
         ps_g = [sb.tile([P, NH], F32, name=f"ps_g{h}") for h in range(2)]
-        for h in range(2):
-            nc.scalar.activation(ps_g[h][:], ps_win[:].indirect(offsets[:, h * NH // 16 : (h + 1) * NH // 16]), ACT.Copy)
+        nc.scalar.activation(ps_g[0][:], ps_win[:].indirect(offsets[:, 0 : NH // 16]), ACT.Copy)
+        nc.scalar.activation(ps_g[1][:, 0:P], ps_win[:].indirect(offsets[:, NH // 16 : (NH + P) // 16]), ACT.Copy)
         ks_g = sb.tile([P, N], U8, name="ks_g", align_bytes=64)
         nc.vector.tensor_copy(ks_g[:], ks_win[:].indirect(offsets[:]))
+        nc.vector.tensor_copy(ps_g[1][:, P:NH], ps_win[:].indirect(offsets[:, (NH + P) // 16 : N // 16]))
         for quad in range(4):
             nc.sync.dma_start(ks_plane[:].bitcast(I32)[32 * quad : 32 * quad + 4, :],
                               ks_g[:].bitcast(I32)[KS0 + 4 * quad : KS0 + 4 * quad + 4, :])

@@ -45,6 +45,7 @@ def tile_attend_plw_alibi_topk_kernel(tc, qT, k_words, k_scales, ps, sl, pq, ls,
         ROW0 = P - NROW
         CUT = 5 * T // 8
         NH = N // 2
+        SHARE = 64
 
         nc.sync.dma_start(offsets[:], offs)
         nc.sync.dma_start(ps_win[P - 1 : P, :], ps[0:1, :])
@@ -78,7 +79,7 @@ def tile_attend_plw_alibi_topk_kernel(tc, qT, k_words, k_scales, ps, sl, pq, ls,
         q_late = late.tile([P, PACK, HALF], F32, name="q_late", offset=0)
         nc.sync.dma_start(q_late[:], q_src[:, :, HALF:NQ])
         q_blocks = [t[:, :, c0 : c0 + QB] for t in (q_first, q_late) for c0 in (0, QB)]
-        at_z = (0, KB, 2 * KB, 3 * KB)
+        at_z = (0, KB, AT_KW + 2 * KB, AT_PEN + 2 * KB)
         kw_g = late.tile([P, N], U32, name="kw_g", offset=AT_PS, align_bytes=64)
         nc.vector.tensor_copy(kw_g[:], kw_win[:].bitcast(U32).indirect(offsets[:]))
 
@@ -99,22 +100,31 @@ def tile_attend_plw_alibi_topk_kernel(tc, qT, k_words, k_scales, ps, sl, pq, ls,
         for c in range(N // P):
             nc.tensor.transpose(ps_bc[:, c * P : (c + 1) * P], ps_col[c].to_broadcast([P, P]), ident[:])
 
-        dist = []
-        for j in range(NB):
-            d = sb.tile([P, 2, P, 2], F32, name=f"dist{j}")
+        def distance(j, d):
             nc.scalar.activation(d[:], ps_bc[:].rearrange("q (s h e) -> q h s e", h=2, e=2), ACT.Abs,
                                  bias=cols[:, NB + j : NB + j + 1], scale=-1.0)
-            dist.append(d)
+            return d
+
+        dist = {j: distance(j, sb.tile([P, 2, P, 2], F32, name=f"dist{j}")) for j in (0, 1, 3)}
 
         q_mx = []
         for j in range(NB):
             qb = late.tile([P, QB, PACK], BF16, name=f"qb{j}", offset=AT_KW + KB * j, align_bytes=64)
-            nc.vector.tensor_copy(qb[:].rearrange("p (c i) t -> p c t i", i=4),
-                                  q_blocks[j].rearrange("p t (c i) -> p c t i", i=4))
-            qw = sb.tile([P, QB], U32, name=f"qw{j}", align_bytes=64)
+            mine = QB if j < NB - 1 else QB - SHARE
+            nc.vector.tensor_copy(qb[:, 0:mine, :].rearrange("p (c i) t -> p c t i", i=4),
+                                  q_blocks[j][:, :, 0:mine].rearrange("p t (c i) -> p c t i", i=4))
+            if mine < QB:
+                nc.scalar.copy(qb[:, mine:QB, :].rearrange("p (c i) t -> p c t i", i=4),
+                               q_blocks[j][:, :, mine:QB].rearrange("p t (c i) -> p c t i", i=4))
+            if j == 2:
+                qw = late.tile([P, QB], U32, name=f"qw{j}", offset=AT_PEN + 2 * KB, align_bytes=64)
+            else:
+                qw = sb.tile([P, QB], U32, name=f"qw{j}", align_bytes=64)
             qs = sb.tile([P, QB], U8, name=f"qs{j}", align_bytes=64)
             nc.vector.quantize_mx(out=qw[:].bitcast(FP8X4), scales=qs[:], in_=qb[:].rearrange("p c t -> p (c t)"))
             q_mx.append((qw, qs))
+
+        dist[2] = distance(2, late.tile([P, 2, P, 2], F32, name="dist2", offset=2 * KB))
 
         score_tags = ("b2", "b3", "b0", "b1")
         pairs = []

from contextlib import ExitStack

import concourse.mybir as mybir

F32 = mybir.dt.float32
BF16 = mybir.dt.bfloat16
I32 = mybir.dt.int32
U32 = mybir.dt.uint32
U16 = mybir.dt.uint16
U8 = mybir.dt.uint8
FP8X4 = mybir.dt.float8_e4m3fn_x4
ACT = mybir.ActivationFunctionType
ALU = mybir.AluOpType

P = 128
PACK = 4
N, T, D, NQ = 512, 2048, 512, 512
QB = 128
NB = NQ // QB
HALF = NQ // 2
FLOPS = 2 * N * D * NQ


def tile_attend_plw_alibi_topk_kernel(tc, qT, k_words, k_scales, ps, sl, pq, ls, offs, out_0, out_1, out_2):
    nc = tc.nc
    with ExitStack() as ctx:
        sb = ctx.enter_context(tc.tile_pool(name="sb", bufs=1))
        late = ctx.enter_context(tc.tile_pool(name="late", bufs=1))
        psum = ctx.enter_context(tc.psum_pool(name="psum", bufs=1))

        KB = 1024
        AT_KS, AT_PS, AT_KW, AT_PEN = 2 * KB, 6 * KB, 14 * KB, 22 * KB
        offsets = sb.tile([P, N // 16], U16, name="offsets")
        ks_win = late.tile([P, T], U8, name="ks_win", offset=AT_KS, align_bytes=64)
        ps_win = late.tile([P, T], F32, name="ps_win", offset=AT_PS)
        kw_win = late.tile([P, T], I32, name="kw_win", offset=AT_KW)
        rows = sb.tile([P, P], F32, name="rows")
        ident = sb.tile([P, P], F32, name="ident")
        warm = sb.tile([P, 8], F32, name="warm")
        ks_plane = sb.tile([P, N], U8, name="ks_plane", align_bytes=64)
        q_src = qT[0].rearrange("(p j) w -> p j w", j=PACK)
        q_first = sb.tile([P, PACK, HALF], F32, name="q_first")
        KS0 = 48
        NROW = 3 * NB
        ROW0 = P - NROW
        CUT = 5 * T // 8
        NH = N // 2
        SHARE = 64

        nc.sync.dma_start(offsets[:], offs)
        nc.sync.dma_start(ps_win[P - 1 : P, :], ps[0:1, :])
        nc.sync.dma_start(ks_win[:].bitcast(I32)[KS0 : KS0 + 16, :], k_scales[0].bitcast(I32))
        for i, vec, eng in ((1, pq, nc.scalar), (0, ls, nc.scalar), (2, sl, nc.sync)):
            eng.dma_start(rows[ROW0 + NB * i : ROW0 + NB * (i + 1), :],
                          vec[0].rearrange("o (c m) -> (o c) m", m=QB))
        nc.sync.dma_start(kw_win[:], k_words[0].rearrange("p t r -> p (t r)").bitcast(I32))
        nc.sync.dma_start(q_first[:], q_src[:, :, 0:HALF])

        nc.vector.memset(rows[0:ROW0, :], 0.0)
        nc.vector.memset(ps_win[0 : P - 1, 0:CUT], 0.0)
        nc.vector.memset(ks_win[:].bitcast(I32)[0:KS0, :], 0)
        nc.gpsimd.memset(ps_win[0 : P - 1, CUT:T], 0.0)
        nc.gpsimd.memset(ks_win[:].bitcast(I32)[64:P, :], 0)
        nc.gpsimd.memset(ident[:], 0.0)
        nc.gpsimd.affine_select(out=ident[:], in_=ident[:], compare_op=ALU.not_equal, fill=1.0, base=0,
                                pattern=[[-1, P]], channel_multiplier=1)
        nc.gpsimd.memset(ks_plane[:].bitcast(I32), 0)
        nc.scalar.activation(warm[0:64, :], rows[0:64, 0:8], ACT.Exp)

        ps_g = [sb.tile([P, NH], F32, name=f"ps_g{h}") for h in range(2)]
        nc.scalar.activation(ps_g[0][:], ps_win[:].indirect(offsets[:, 0 : NH // 16]), ACT.Copy)
        nc.scalar.activation(ps_g[1][:, 0:P], ps_win[:].indirect(offsets[:, NH // 16 : (NH + P) // 16]), ACT.Copy)
        ks_g = sb.tile([P, N], U8, name="ks_g", align_bytes=64)
        nc.vector.tensor_copy(ks_g[:], ks_win[:].indirect(offsets[:]))
        nc.vector.tensor_copy(ps_g[1][:, P:NH], ps_win[:].indirect(offsets[:, (NH + P) // 16 : N // 16]))
        for quad in range(4):
            nc.sync.dma_start(ks_plane[:].bitcast(I32)[32 * quad : 32 * quad + 4, :],
                              ks_g[:].bitcast(I32)[KS0 + 4 * quad : KS0 + 4 * quad + 4, :])
        q_late = late.tile([P, PACK, HALF], F32, name="q_late", offset=0)
        nc.sync.dma_start(q_late[:], q_src[:, :, HALF:NQ])
        q_blocks = [t[:, :, c0 : c0 + QB] for t in (q_first, q_late) for c0 in (0, QB)]
        at_z = (0, KB, AT_KW + 2 * KB, AT_PEN + 2 * KB)
        kw_g = late.tile([P, N], U32, name="kw_g", offset=AT_PS, align_bytes=64)
        nc.vector.tensor_copy(kw_g[:], kw_win[:].bitcast(U32).indirect(offsets[:]))

        turned = psum.tile([P, 2, P], F32, name="turned", tag="b0")
        for c in range(2):
            nc.tensor.transpose(turned[:, c, :], ps_g[0][:, c * P : (c + 1) * P], ident[:])
        head = sb.tile([P, 2], F32, name="head")
        nc.scalar.copy(head[:], turned[:, :, P - 1])
        turned2 = psum.tile([P, 3, P], F32, name="turned2", tag="b1")
        nc.tensor.transpose(turned2[:, 2, :], rows[:], ident[:])
        for c in range(2):
            nc.tensor.transpose(turned2[:, c, :], ps_g[1][:, c * P : (c + 1) * P], ident[:])
        rest = sb.tile([P, 3, NROW], F32, name="rest")
        nc.scalar.copy(rest[:], turned2[:, :, ROW0:P])
        cols = rest[:, 2, :]
        ps_col = [head[:, 0:1], head[:, 1:2], rest[:, 0, NROW - 1 : NROW], rest[:, 1, NROW - 1 : NROW]]
        ps_bc = psum.tile([P, N], F32, name="ps_bc", tag="o3")
        for c in range(N // P):
            nc.tensor.transpose(ps_bc[:, c * P : (c + 1) * P], ps_col[c].to_broadcast([P, P]), ident[:])

        def distance(j, d):
            nc.scalar.activation(d[:], ps_bc[:].rearrange("q (s h e) -> q h s e", h=2, e=2), ACT.Abs,
                                 bias=cols[:, NB + j : NB + j + 1], scale=-1.0)
            return d

        dist = {j: distance(j, sb.tile([P, 2, P, 2], F32, name=f"dist{j}")) for j in (0, 1, 3)}

        q_mx = []
        for j in range(NB):
            qb = late.tile([P, QB, PACK], BF16, name=f"qb{j}", offset=AT_KW + KB * j, align_bytes=64)
            mine = QB if j < NB - 1 else QB - SHARE
            nc.vector.tensor_copy(qb[:, 0:mine, :].rearrange("p (c i) t -> p c t i", i=4),
                                  q_blocks[j][:, :, 0:mine].rearrange("p t (c i) -> p c t i", i=4))
            if mine < QB:
                nc.scalar.copy(qb[:, mine:QB, :].rearrange("p (c i) t -> p c t i", i=4),
                               q_blocks[j][:, :, mine:QB].rearrange("p t (c i) -> p c t i", i=4))
            if j == 2:
                qw = late.tile([P, QB], U32, name=f"qw{j}", offset=AT_PEN + 2 * KB, align_bytes=64)
            else:
                qw = sb.tile([P, QB], U32, name=f"qw{j}", align_bytes=64)
            qs = sb.tile([P, QB], U8, name=f"qs{j}", align_bytes=64)
            nc.vector.quantize_mx(out=qw[:].bitcast(FP8X4), scales=qs[:], in_=qb[:].rearrange("p c t -> p (c t)"))
            q_mx.append((qw, qs))

        dist[2] = distance(2, late.tile([P, 2, P, 2], F32, name="dist2", offset=2 * KB))

        score_tags = ("b2", "b3", "b0", "b1")
        pairs = []
        for j in range(NB):
            qw, qs = q_mx[j]
            a = psum.tile([P, N], F32, name=f"a{j}", tag=score_tags[j])
            nc.tensor.matmul_mx(out=a[:], lhsT=qw[:].bitcast(FP8X4), lhsT_scale=qs[:],
                                rhs=kw_g[:].bitcast(FP8X4), rhs_scale=ks_plane[:], start=True, stop=True)
            pairs.append(a[:].rearrange("q (s h e) -> q h s e", h=2, e=2))

        acc = {(0, h): psum.tile([P, 2, HALF], F32, name=f"acc0_{h}", tag=f"o{h}") for h in range(2)}
        for h in range(2):
            for j in range(2):
                ls_col = cols[:, j : j + 1].to_broadcast([P, P])
                for e in range(2):
                    nc.tensor.matmul(acc[0, h][:, e, j * QB : (j + 1) * QB], ls_col, ident[:], is_transpose=True,
                                     start=(j == 0 and e == 0), stop=False)
        pen = {}
        for j in range(2, NB):
            pen[j] = late.tile([P, 2, P, 2], F32, name=f"pen{j}", offset=AT_PEN if j == 2 else AT_KW + 3 * KB,
                               align_bytes=64)
        nc.scalar.activation(pen[2][:], dist[2][:], ACT.Identity, bias=cols[:, 2:3],
                             scale=cols[:, 2 * NB + 2 : 2 * NB + 3])
        nc.gpsimd.tensor_scalar(pen[3][:].rearrange("q h s e -> q (h s e)"), dist[3][:].rearrange("q h s e -> q (h s e)"),
                                cols[:, 2 * NB + 3 : 2 * NB + 4], cols[:, 3:4], ALU.mult, ALU.add)

        y_words = sb.tile([P, NQ], U32, name="y_words", align_bytes=64)
        y_scales = sb.tile([P, NQ], U8, name="y_scales", align_bytes=64)
        out_rows = out_0.rearrange("(s r) q -> s r q", r=PACK)
        out_words = out_1[0].rearrange("p q u -> p (q u)").bitcast(I32)

        y = [sb.tile([P, PACK, HALF], F32, name=f"y{g}") for g in range(2)]

        for h in range(2):
            for j in range(2):
                z = late.tile([P, 2, P], F32, name=f"z{j}_{h}", offset=at_z[2 * h + j])
                nc.vector.scalar_tensor_tensor(z[:].rearrange("q e s -> q s e"), dist[j][:, h],
                                               cols[:, 2 * NB + j : 2 * NB + j + 1], pairs[j][:, h],
                                               ALU.mult, ALU.subtract)
                for e in range(2):
                    nc.tensor.matmul(acc[0, h][:, e, j * QB : (j + 1) * QB], z[:, e, :], ident[:],
                                     is_transpose=True, start=False, stop=(j == 1 and e == 1))
            nc.scalar.activation(y[0][:, 2 * h : 2 * h + 2, :], acc[0, h][:], ACT.Exp, scale=-1.0)
            nc.sync.dma_start(out_rows[:, 2 * h : 2 * h + 2, 0:HALF], y[0][:, 2 * h : 2 * h + 2, :])
        for j in range(2, NB):
            turned_back = psum.tile([P, PACK, QB], F32, name=f"acc{j}", tag=f"o{j}")
            for h in range(2):
                z = sb.tile([P, 2, P], F32, name=f"z{j}_{h}")
                nc.vector.tensor_tensor(z[:].rearrange("q e s -> q s e"), pen[j][:, h], pairs[j][:, h], ALU.subtract)
                for e in range(2):
                    nc.tensor.transpose(turned_back[:, 2 * h + e, :], z[:, e, :], ident[:])
            nc.scalar.activation(y[1][:, :, (j - 2) * QB : (j - 1) * QB], turned_back[:], ACT.Exp, scale=-1.0)
        nc.scalar.dma_start(out_rows[:, :, HALF:NQ], y[1][:])
        for j in range(NB):
            cs = slice(j * QB, (j + 1) * QB)
            g, c0 = divmod(j * QB, HALF)
            yb = late.tile([P, QB, PACK], BF16, name=f"yb{j}", offset=AT_KW + (3 + j) * KB, align_bytes=64)
            nc.vector.tensor_copy(yb[:].rearrange("p (c i) t -> p c t i", i=4),
                                  y[g][:, :, c0 : c0 + QB].rearrange("p t (c i) -> p c t i", i=4))
            nc.vector.quantize_mx(out=y_words[:, cs].bitcast(FP8X4), scales=y_scales[:, cs],
                                  in_=yb[:].rearrange("p c t -> p (c t)"))
            if j % 2:
                hs = slice((j - 1) * QB, (j + 1) * QB)
                nc.sync.dma_start(out_words[:, hs], y_words[:, hs].bitcast(I32))
        for quad in range(4):
            eng = nc.scalar if quad % 2 else nc.sync
            eng.dma_start(out_2[0, 4 * quad : 4 * quad + 4, :].bitcast(I32),
                          y_scales[:].bitcast(I32)[32 * quad : 32 * quad + 4, :])
